import numpy as np
import ml_dtypes


def mxq(x, axis, fmt="e4m3"):
    dtype, down = {"e4m3": (ml_dtypes.float8_e4m3fn, 7), "e5m2": (ml_dtypes.float8_e5m2, 14)}[fmt]
    v = np.moveaxis(np.asarray(x, np.float32).astype(ml_dtypes.bfloat16).astype(np.float64), axis, -1)
    blocks = v.reshape(v.shape[:-1] + (-1, 32))
    amax = np.abs(blocks).max(-1, keepdims=True)
    byte = np.maximum(np.where(amax > 0, np.frexp(amax)[1] - 1 + 127, 0) - down, 1)
    scale = np.exp2(byte - 127.0)
    codes = (blocks / scale).astype(np.float32).astype(dtype).astype(np.float64)
    return np.moveaxis((codes * scale).reshape(v.shape), -1, axis)


WIDE = False


def mx_kscale(k):
    if not WIDE:
        return np.ones(k)
    levels = np.array([10, -10, 5, -5, 0])
    if k % 512:
        return np.exp2(np.random.permutation(np.resize(levels, k // 32))).repeat(32)
    a = np.empty((k // 512, 16))
    for p in range(k // 512):
        a[p, :8] = np.random.permutation(np.resize(levels, 8))
        for g in range(8):
            far = levels[np.abs(levels - a[p, g]) >= 10]
            a[p, g + 8] = far[np.random.randint(len(far))]
    return np.exp2(a.ravel()).repeat(32)


def f64(x):
    return np.asarray(x).astype(np.float64)


def striped(idx):
    return np.tile(np.asarray(idx).reshape(-1, 16).T, (8, 1)).astype(np.uint16)


def unstriped(offs):
    return offs[:16].T.reshape(-1).astype(np.int64)


def striped8(idx):
    return np.asarray(idx).reshape(8, -1, 16).transpose(0, 2, 1).reshape(128, -1).astype(np.uint16)


def unstriped8(offs):
    return offs.reshape(8, 16, -1).transpose(0, 2, 1).reshape(8, -1).astype(np.int64)


def pick8(x, idx, run):
    r = np.arange(len(x))
    return x[r[:, None], idx[r % (8 * run) // run]]


E2M1 = np.array([0.0, 0.5, 1.0, 1.5, 2.0, 3.0, 4.0, 6.0, -0.0, -0.5, -1.0, -1.5, -2.0, -3.0, -4.0, -6.0])


def pack_weight(w, fmt):
    k, n = w.shape
    w = f64(np.asarray(w, np.float32).astype(ml_dtypes.bfloat16)).reshape(k // 32, 32, n)
    amax = np.abs(w).max(1)
    if fmt == "e4m3":
        byte = np.frexp(amax)[1] - 1 + 127 - 7
    else:
        mant, ex = np.frexp(amax / 6.0)
        byte = np.where(mant > 0.5, ex, ex - 1) + 127
    byte = np.clip(np.where(amax > 0, byte, 1), 1, 254)
    scaled = (w * np.exp2(127.0 - byte)[:, None, :]).reshape(k, n).astype(np.float32)
    by_word = np.ascontiguousarray(scaled.reshape(k // 512, 128, 4, n).transpose(0, 1, 3, 2))
    if fmt == "e4m3":
        words = by_word.astype(ml_dtypes.float8_e4m3fn).view(np.uint8)
    else:
        c = by_word.astype(ml_dtypes.float4_e2m1fn).view(np.uint8) & 0xF
        words = (c[..., 0::2] | (c[..., 1::2] << 4)).reshape(k // 512, 128, 2 * n)
    return np.ascontiguousarray(words), np.ascontiguousarray(byte.astype(np.uint8).reshape(k // 512, 16, n))


def unpack_weight(words, scales, fmt):
    g, _, n = scales.shape
    words = np.ascontiguousarray(words).reshape(g, 128, n, -1)
    if fmt == "e4m3":
        vals = words.view(ml_dtypes.float8_e4m3fn).astype(np.float64)
    else:
        nib = np.empty((g, 128, n, 4), np.uint8)
        nib[..., 0::2] = words & 0xF
        nib[..., 1::2] = words >> 4
        vals = E2M1[nib]
    vals = vals * np.repeat(np.exp2(scales.astype(np.float64) - 127.0), 8, axis=1)[..., None]
    return vals.transpose(0, 1, 3, 2).reshape(g * 512, n)


K, J, R, T, F, O, C, N = 512, 512, 512, 2048, 2048, 256, 1024, 256


def setup_inputs():
    n = np.random.standard_normal
    idx = np.random.permutation(T)[:J]
    idx2 = np.stack([np.random.permutation(F)[:R] for _ in range(8)])
    idx3 = np.stack([np.random.permutation(C)[:J] for _ in range(8)])
    idx4 = np.stack([np.random.permutation(C)[:O] for _ in range(8)])
    idx5 = np.stack([np.random.permutation(C)[:O] for _ in range(8)])
    fk = mx_kscale(K)
    fr = mx_kscale(R)
    xtp = pack_weight(n((K, T)) * fk[:, None], "e4m3")
    wbp = pack_weight(n((R, N)) * 1 / np.sqrt(R) / fr[:, None], "e4m3")
    return {
        "xt_words": xtp[0],
        "xt_scales": xtp[1],
        "ua": (np.random.randint(-7, 8, (K, F)).astype(np.float64)).astype(np.float32),
        "ha": ((np.random.randint(8, 25, (K, 1)) / 1024.0) / fk[:, None]).astype(np.float32),
        "sa": (np.random.uniform(0.5, 1.6, (R, 1)) * fr[:, None]).astype(np.float32),
        "sb": (np.random.uniform(0.5, 1.6, (R, 1)) * fr[:, None]).astype(np.float32),
        "wb_words": wbp[0],
        "wb_scales": wbp[1],
        "offs": striped(idx),
        "offs2": striped8(idx2),
        "offs3": striped8(idx3),
        "offs4": striped8(idx4),
        "offs5": striped8(idx5),
    }


def reference(xt_words, xt_scales, ua, ha, sa, sb, wb_words, wb_scales, offs, offs2, offs3, offs4, offs5):
    idx = unstriped(offs)
    idx2 = unstriped8(offs2)
    idx3 = unstriped8(offs3)
    idx4 = unstriped8(offs4)
    idx5 = unstriped8(offs5)
    xtu = unpack_weight(xt_words, xt_scales, "e4m3")
    wbu = unpack_weight(wb_words, wb_scales, "e4m3")
    wc = pick8(f64(ua), idx2, 64) * f64(ha)
    wcq = mxq(wc, 0, "e4m3")
    xtidxg = xtu[:, idx]
    a = wcq.T @ xtidxg
    pw = np.zeros((R, C))
    pw[np.arange(R)[:, None], idx3[np.arange(R) % 512 // 64]] = a
    hid = np.maximum(pick8(pw, idx4, 64) * f64(sa), pick8(pw, idx5, 64) * f64(sb))
    hidq = mxq(hid, 0, "e4m3")
    y = wbu.T @ hidq
    return y

@@ -1,0 +1,170 @@
+from contextlib import ExitStack
+
+import concourse.mybir as mybir
+
+K, J, R, T, F, O, C, N = 512, 512, 512, 2048, 2048, 256, 1024, 256
+FLOPS = 2 * K * R * J + 2 * R * N * O
+
+F32 = mybir.dt.float32
+BF16 = mybir.dt.bfloat16
+I32 = mybir.dt.int32
+U32 = mybir.dt.uint32
+U16 = mybir.dt.uint16
+U8 = mybir.dt.uint8
+FP8X4 = mybir.dt.float8_e4m3fn_x4
+COPY = mybir.ActivationFunctionType.Copy
+MAX = mybir.AluOpType.max
+
+P = 128
+PACK = 4
+HALF = J // 2
+
+
+def tile_picked_tokens_codes_one_boardpair_one_plain_kernel(
+    tc, xt_words, xt_scales, ua, ha, sa, sb, wb_words, wb_scales, offs, offs2, offs3, offs4, offs5, out
+):
+    nc = tc.nc
+    with ExitStack() as ctx:
+        keep = ctx.enter_context(tc.tile_pool(name="keep", bufs=1))
+        psum = ctx.enter_context(tc.psum_pool(name="psum", bufs=1))
+
+        token_list = keep.tile([P, J // 16], U16, name="token_list")
+        code_list = keep.tile([P, R // 16], U16, name="code_list")
+        board_list = keep.tile([P, J // 16], U16, name="board_list")
+        first_list = keep.tile([P, O // 16], U16, name="first_list")
+        second_list = keep.tile([P, O // 16], U16, name="second_list")
+
+        ha_sb = keep.tile([P, PACK], F32, name="ha_sb")
+        sa_sb = keep.tile([P, PACK], F32, name="sa_sb")
+        sb_sb = keep.tile([P, PACK], F32, name="sb_sb")
+        tables = [keep.tile([P, F], F32, name=f"table{t}") for t in range(PACK)]
+        xt_word_table = keep.tile([P, T], I32, name="xt_word_table")
+        xt_scale_table = keep.tile([P, T], U8, name="xt_scale_table")
+        wb_codes = keep.tile([P, N], I32, name="wb_codes", align_bytes=64)
+        wb_plane = keep.tile([P, N], U8, name="wb_plane", align_bytes=64)
+        boards = [keep.tile([P, C], F32, name=f"board{t}") for t in range(PACK)]
+
+        nc.gpsimd.memset(xt_scale_table[:].bitcast(I32), 0)
+        x_plane = keep.tile([P, J], U8, name="x_plane", align_bytes=64)
+        nc.gpsimd.memset(x_plane[:].bitcast(I32), 0)
+        nc.gpsimd.memset(wb_plane[:].bitcast(I32), 0)
+        for t in range(PACK):
+            nc.vector.memset(boards[t][:], 0.0)
+
+        ua_rows = ua.rearrange("(p t) f -> p t f", t=PACK)
+        xt_scale_rows = xt_scales[0].bitcast(I32)
+        wb_scale_rows = wb_scales[0].bitcast(I32)
+
+        nc.sync.dma_start(tables[0][:], ua_rows[:, 0, :])
+        nc.sync.dma_start(code_list[:], offs2)
+        nc.scalar.dma_start(ha_sb[:], ha.rearrange("(p t) one -> p (t one)", t=PACK))
+        nc.sync.dma_start(token_list[:], offs)
+        nc.sync.dma_start(xt_scale_table[0:P:8, :].bitcast(I32), xt_scale_rows)
+        for t in range(1, PACK):
+            nc.sync.dma_start(tables[t][:], ua_rows[:, t, :])
+        nc.sync.dma_start(xt_word_table[:], xt_words[0].rearrange("p c t -> p (c t)").bitcast(I32))
+        nc.sync.dma_start(board_list[:], offs3)
+        nc.sync.dma_start(first_list[:], offs4)
+        nc.sync.dma_start(second_list[:], offs5)
+        nc.sync.dma_start(sa_sb[:], sa.rearrange("(p t) one -> p (t one)", t=PACK))
+        nc.sync.dma_start(sb_sb[:], sb.rearrange("(p t) one -> p (t one)", t=PACK))
+        nc.sync.dma_start(wb_codes[:], wb_words[0].rearrange("p n t -> p (n t)").bitcast(I32))
+        for i in range(4):
+            nc.sync.dma_start(wb_plane[i:P:32, :].bitcast(I32), wb_scale_rows[i:16:4, :])
+
+        x_scales = keep.tile([P, J], U8, name="x_scales")
+        nc.vector.tensor_copy(x_scales[:], xt_scale_table[:].indirect(token_list[:]))
+        for i in range(4):
+            nc.gpsimd.dma_start(x_plane[i:P:32, :].bitcast(I32), x_scales[8 * i : P : 32, :].bitcast(I32))
+
+        wc = keep.tile([P, PACK, R], BF16, name="wc")
+        for t in range(PACK):
+            nc.scalar.activation(
+                out=wc[:, t, :], in_=tables[t][:].indirect(code_list[:]), func=COPY, scale=ha_sb[:, t : t + 1]
+            )
+
+        dealt = wc[:].rearrange("p j (m t) -> p t m j", t=PACK)
+        grouped = [keep.tile([P, 2, P, PACK], BF16, name=f"grouped{u}", align_bytes=64) for u in range(2)]
+        w_codes = [keep.tile([P, 2 * P], U32, name=f"w_codes{u}", align_bytes=64) for u in range(2)]
+        w_plane = [keep.tile([P, 2 * P], U8, name=f"w_plane{u}", align_bytes=64) for u in range(2)]
+
+        def quantize_w(u):
+            nc.vector.quantize_mx(
+                out=w_codes[u][:].bitcast(FP8X4),
+                scales=w_plane[u][:],
+                in_=grouped[u][:].rearrange("p t m j -> p (t m j)"),
+            )
+
+        nc.vector.tensor_copy(grouped[0][:], dealt[:, 0:2])
+        nc.scalar.copy(grouped[1][:], dealt[:, 2:4])
+        quantize_w(0)
+
+        x_codes = keep.tile([P, J], U32, name="x_codes", align_bytes=64)
+        for h in range(2):
+            nc.vector.tensor_copy(
+                x_codes[:, h * HALF : (h + 1) * HALF],
+                xt_word_table[:].bitcast(U32).indirect(token_list[:, h * HALF // 16 : (h + 1) * HALF // 16]),
+            )
+        quantize_w(1)
+
+        first = [keep.tile([P, 2, O], F32, name=f"first{u}") for u in range(2)]
+        second = [keep.tile([P, 2, O], F32, name=f"second{u}") for u in range(2)]
+        spans = [[(0, HALF), (HALF, J)]] + [[(0, J)]] * (PACK - 1)
+        a_sb = [keep.tile([P, J], F32, name=f"a_sb{t}", tag=f"a_sb{t}", align_bytes=64) for t in range(PACK)]
+        for t in range(PACK):
+            u, v = divmod(t, 2)
+            for j0, j1 in spans[t]:
+                acc = psum.tile([P, j1 - j0], F32, name=f"acc{t}_{j0}")
+                nc.tensor.matmul_mx(
+                    out=acc[:],
+                    lhsT=w_codes[u][:, v * P : (v + 1) * P].bitcast(FP8X4),
+                    lhsT_scale=w_plane[u][:, v * P : (v + 1) * P],
+                    rhs=x_codes[:, j0:j1].bitcast(FP8X4),
+                    rhs_scale=x_plane[:, j0:j1],
+                    start=True,
+                    stop=True,
+                )
+                nc.scalar.copy(a_sb[t][:, j0:j1], acc[:])
+        for t in range(PACK):
+            u, v = divmod(t, 2)
+            for j0, j1 in spans[t]:
+                nc.vector.tensor_copy(boards[t][:].indirect(board_list[:, j0 // 16 : j1 // 16]), a_sb[t][:, j0:j1])
+            nc.scalar.activation(
+                out=first[u][:, v, :], in_=boards[t][:].indirect(first_list[:]), func=COPY, scale=sa_sb[:, t : t + 1]
+            )
+            nc.scalar.activation(
+                out=second[u][:, v, :], in_=boards[t][:].indirect(second_list[:]), func=COPY, scale=sb_sb[:, t : t + 1]
+            )
+
+        hid = keep.tile([P, O, PACK], BF16, name="hid", tag=f"a_sb{PACK - 1}", align_bytes=64)
+        for u in range(2):
+            nc.vector.tensor_tensor(
+                hid[:, :, 2 * u : 2 * u + 2],
+                first[u][:].rearrange("p v o -> p o v"),
+                second[u][:].rearrange("p v o -> p o v"),
+                MAX,
+            )
+        h_codes = keep.tile([P, O], U32, name="h_codes", align_bytes=64)
+        h_plane = keep.tile([P, O], U8, name="h_plane", align_bytes=64)
+        nc.vector.quantize_mx(
+            out=h_codes[:].bitcast(FP8X4), scales=h_plane[:], in_=hid[:].rearrange("p o t -> p (o t)")
+        )
+
+        for b in range(N // P):
+            y = psum.tile([P, O], F32, name=f"y{b}")
+            nc.tensor.matmul_mx(
+                out=y[:],
+                lhsT=wb_codes[:, b * P : (b + 1) * P].bitcast(FP8X4),
+                lhsT_scale=wb_plane[:, b * P : (b + 1) * P],
+                rhs=h_codes[:].bitcast(FP8X4),
+                rhs_scale=h_plane[:],
+                start=True,
+                stop=True,
+            )
+            y_sb = keep.tile([P, O], F32, name=f"y_sb{b}")
+            if b == 0:
+                nc.vector.tensor_copy(y_sb[:], y[:])
+                nc.sync.dma_start(out[b * P : (b + 1) * P, :], y_sb[:])
+            else:
+                nc.scalar.copy(y_sb[:], y[:])
+                nc.scalar.dma_start(out[b * P : (b + 1) * P, :], y_sb[:])

@@ -17,7 +17,6 @@ MAX = mybir.AluOpType.max
 
 P = 128
 PACK = 4
-HALF = J // 2
 
 
 def tile_picked_tokens_codes_one_boardpair_one_plain_kernel(
@@ -45,8 +44,6 @@ def tile_picked_tokens_codes_one_boardpair_one_plain_kernel(
         boards = [keep.tile([P, C], F32, name=f"board{t}") for t in range(PACK)]
 
         nc.gpsimd.memset(xt_scale_table[:].bitcast(I32), 0)
-        x_plane = keep.tile([P, J], U8, name="x_plane", align_bytes=64)
-        nc.gpsimd.memset(x_plane[:].bitcast(I32), 0)
         nc.gpsimd.memset(wb_plane[:].bitcast(I32), 0)
         for t in range(PACK):
             nc.vector.memset(boards[t][:], 0.0)
@@ -74,42 +71,60 @@ def tile_picked_tokens_codes_one_boardpair_one_plain_kernel(
 
         x_scales = keep.tile([P, J], U8, name="x_scales")
         nc.vector.tensor_copy(x_scales[:], xt_scale_table[:].indirect(token_list[:]))
-        for i in range(4):
+        x_plane = keep.tile([P, J], U8, name="x_plane", align_bytes=64)
+        nc.vector.tensor_copy(x_plane[:], x_scales[:])
+        for i in range(1, 4):
             nc.gpsimd.dma_start(x_plane[i:P:32, :].bitcast(I32), x_scales[8 * i : P : 32, :].bitcast(I32))
 
-        wc = keep.tile([P, PACK, R], BF16, name="wc")
-        for t in range(PACK):
-            nc.scalar.activation(
-                out=wc[:, t, :], in_=tables[t][:].indirect(code_list[:]), func=COPY, scale=ha_sb[:, t : t + 1]
-            )
-
-        dealt = wc[:].rearrange("p j (m t) -> p t m j", t=PACK)
-        grouped = [keep.tile([P, 2, P, PACK], BF16, name=f"grouped{u}", align_bytes=64) for u in range(2)]
+        wc = [keep.tile([P, 2, R], BF16, name=f"wc{e}") for e in range(2)]
+        grouped = [keep.tile([P, 2 * P * PACK], BF16, name=f"grouped{u}", align_bytes=64) for u in range(2)]
         w_codes = [keep.tile([P, 2 * P], U32, name=f"w_codes{u}", align_bytes=64) for u in range(2)]
         w_plane = [keep.tile([P, 2 * P], U8, name=f"w_plane{u}", align_bytes=64) for u in range(2)]
 
-        def quantize_w(u):
+        def gather_w(j):
+            nc.scalar.activation(
+                out=wc[j // 2][:, j % 2, :],
+                in_=tables[j][:].indirect(code_list[:]),
+                func=COPY,
+                scale=ha_sb[:, j : j + 1],
+            )
+
+        def weave(copy, e, t0, t1):
+            u, v = divmod(t0, 2)
+            words = grouped[u][:, v * P * PACK : (v + t1 - t0) * P * PACK].rearrange("p (t m j) -> p t m j", m=P, j=PACK)
+            copy(words[:, :, :, 2 * e : 2 * e + 2], wc[e][:].rearrange("p j (m t) -> p t m j", t=PACK)[:, t0:t1])
+
+        def quantize_w(t0, t1):
+            u, v = divmod(t0, 2)
             nc.vector.quantize_mx(
-                out=w_codes[u][:].bitcast(FP8X4),
-                scales=w_plane[u][:],
-                in_=grouped[u][:].rearrange("p t m j -> p (t m j)"),
+                out=w_codes[u][:, v * P : (v + t1 - t0) * P].bitcast(FP8X4),
+                scales=w_plane[u][:, v * P : (v + t1 - t0) * P],
+                in_=grouped[u][:, v * P * PACK : (v + t1 - t0) * P * PACK],
             )
 
-        nc.vector.tensor_copy(grouped[0][:], dealt[:, 0:2])
-        nc.scalar.copy(grouped[1][:], dealt[:, 2:4])
-        quantize_w(0)
+        gather_w(0)
+        gather_w(1)
+        weave(nc.vector.tensor_copy, 0, 0, 2)
+        weave(nc.vector.tensor_copy, 0, 2, 4)
+        gather_w(2)
+        gather_w(3)
+        weave(nc.vector.tensor_copy, 1, 0, 1)
+        weave(nc.vector.tensor_copy, 1, 1, 2)
+        weave(nc.scalar.copy, 1, 2, 4)
+        quantize_w(0, 1)
+        quantize_w(1, 2)
 
+        first_spans = [(0, 128), (128, 256), (256, 512)]
         x_codes = keep.tile([P, J], U32, name="x_codes", align_bytes=64)
-        for h in range(2):
+        for j0, j1 in first_spans:
             nc.vector.tensor_copy(
-                x_codes[:, h * HALF : (h + 1) * HALF],
-                xt_word_table[:].bitcast(U32).indirect(token_list[:, h * HALF // 16 : (h + 1) * HALF // 16]),
+                x_codes[:, j0:j1], xt_word_table[:].bitcast(U32).indirect(token_list[:, j0 // 16 : j1 // 16])
             )
-        quantize_w(1)
+        quantize_w(2, 4)
 
         first = [keep.tile([P, 2, O], F32, name=f"first{u}") for u in range(2)]
         second = [keep.tile([P, 2, O], F32, name=f"second{u}") for u in range(2)]
-        spans = [[(0, HALF), (HALF, J)]] + [[(0, J)]] * (PACK - 1)
+        spans = [first_spans] + [[(0, J)]] * (PACK - 1)
         a_sb = [keep.tile([P, J], F32, name=f"a_sb{t}", tag=f"a_sb{t}", align_bytes=64) for t in range(PACK)]
         for t in range(PACK):
             u, v = divmod(t, 2)
@@ -136,35 +151,44 @@ def tile_picked_tokens_codes_one_boardpair_one_plain_kernel(
                 out=second[u][:, v, :], in_=boards[t][:].indirect(second_list[:]), func=COPY, scale=sb_sb[:, t : t + 1]
             )
 
-        hid = keep.tile([P, O, PACK], BF16, name="hid", tag=f"a_sb{PACK - 1}", align_bytes=64)
-        for u in range(2):
+        hid = keep.tile([P, O * PACK], BF16, name="hid", tag=f"a_sb{PACK - 1}", align_bytes=64)
+
+        def larger(u, o0, o1):
             nc.vector.tensor_tensor(
-                hid[:, :, 2 * u : 2 * u + 2],
-                first[u][:].rearrange("p v o -> p o v"),
-                second[u][:].rearrange("p v o -> p o v"),
+                hid[:, o0 * PACK : o1 * PACK].rearrange("p (o t) -> p o t", t=PACK)[:, :, 2 * u : 2 * u + 2],
+                first[u][:, :, o0:o1].rearrange("p v o -> p o v"),
+                second[u][:, :, o0:o1].rearrange("p v o -> p o v"),
                 MAX,
             )
+
+        halves = [(0, O // 2), (O // 2, O)]
+        larger(0, 0, O)
+        for o0, o1 in halves:
+            larger(1, o0, o1)
         h_codes = keep.tile([P, O], U32, name="h_codes", align_bytes=64)
         h_plane = keep.tile([P, O], U8, name="h_plane", align_bytes=64)
-        nc.vector.quantize_mx(
-            out=h_codes[:].bitcast(FP8X4), scales=h_plane[:], in_=hid[:].rearrange("p o t -> p (o t)")
-        )
-
-        for b in range(N // P):
-            y = psum.tile([P, O], F32, name=f"y{b}")
-            nc.tensor.matmul_mx(
-                out=y[:],
-                lhsT=wb_codes[:, b * P : (b + 1) * P].bitcast(FP8X4),
-                lhsT_scale=wb_plane[:, b * P : (b + 1) * P],
-                rhs=h_codes[:].bitcast(FP8X4),
-                rhs_scale=h_plane[:],
-                start=True,
-                stop=True,
+        for o0, o1 in halves:
+            nc.vector.quantize_mx(
+                out=h_codes[:, o0:o1].bitcast(FP8X4), scales=h_plane[:, o0:o1], in_=hid[:, o0 * PACK : o1 * PACK]
             )
-            y_sb = keep.tile([P, O], F32, name=f"y_sb{b}")
-            if b == 0:
-                nc.vector.tensor_copy(y_sb[:], y[:])
-                nc.sync.dma_start(out[b * P : (b + 1) * P, :], y_sb[:])
-            else:
+
+        out_rows = out.rearrange("(b p) o -> p b o", p=P)
+        for h, (o0, o1) in enumerate(halves):
+            y = psum.tile([P, N // P, o1 - o0], F32, name=f"y{h}")
+            for b in range(N // P):
+                nc.tensor.matmul_mx(
+                    out=y[:, b, :],
+                    lhsT=wb_codes[:, b * P : (b + 1) * P].bitcast(FP8X4),
+                    lhsT_scale=wb_plane[:, b * P : (b + 1) * P],
+                    rhs=h_codes[:, o0:o1].bitcast(FP8X4),
+                    rhs_scale=h_plane[:, o0:o1],
+                    start=True,
+                    stop=True,
+                )
+            y_sb = keep.tile([P, N // P, o1 - o0], F32, name=f"y_sb{h}")
+            if h == 0:
                 nc.scalar.copy(y_sb[:], y[:])
-                nc.scalar.dma_start(out[b * P : (b + 1) * P, :], y_sb[:])
+                nc.scalar.dma_start(out_rows[:, :, o0:o1], y_sb[:])
+            else:
+                nc.vector.tensor_copy(y_sb[:], y[:])
+                nc.sync.dma_start(out_rows[:, :, o0:o1], y_sb[:])

@@ -17,6 +17,7 @@ MAX = mybir.AluOpType.max
 
 P = 128
 PACK = 4
+HEAD = 128
 
 
 def tile_picked_tokens_codes_one_boardpair_one_plain_kernel(
@@ -114,42 +115,52 @@ def tile_picked_tokens_codes_one_boardpair_one_plain_kernel(
         quantize_w(0, 1)
         quantize_w(1, 2)
 
-        first_spans = [(0, 128), (128, 256), (256, 512)]
+        head, rest, whole = (0, HEAD), (HEAD, J), (0, J)
         x_codes = keep.tile([P, J], U32, name="x_codes", align_bytes=64)
-        for j0, j1 in first_spans:
+        for j0, j1 in (head, rest):
             nc.vector.tensor_copy(
                 x_codes[:, j0:j1], xt_word_table[:].bitcast(U32).indirect(token_list[:, j0 // 16 : j1 // 16])
             )
         quantize_w(2, 4)
 
-        first = [keep.tile([P, 2, O], F32, name=f"first{u}") for u in range(2)]
-        second = [keep.tile([P, 2, O], F32, name=f"second{u}") for u in range(2)]
-        spans = [first_spans] + [[(0, J)]] * (PACK - 1)
+        pieces = [(0, head), (1, head), (0, rest), (1, rest), (2, whole), (3, whole)]
+        widths = {head: [128], rest: [128, 256], whole: [512]}
         a_sb = [keep.tile([P, J], F32, name=f"a_sb{t}", tag=f"a_sb{t}", align_bytes=64) for t in range(PACK)]
-        for t in range(PACK):
+        for bank, (t, (j0, j1)) in enumerate(pieces):
             u, v = divmod(t, 2)
-            for j0, j1 in spans[t]:
-                acc = psum.tile([P, j1 - j0], F32, name=f"acc{t}_{j0}")
+            acc = psum.tile([P, j1 - j0], F32, name=f"acc{bank}", tag=f"bank{bank}")
+            c0 = j0
+            for width in widths[(j0, j1)]:
                 nc.tensor.matmul_mx(
-                    out=acc[:],
+                    out=acc[:, c0 - j0 : c0 - j0 + width],
                     lhsT=w_codes[u][:, v * P : (v + 1) * P].bitcast(FP8X4),
                     lhsT_scale=w_plane[u][:, v * P : (v + 1) * P],
-                    rhs=x_codes[:, j0:j1].bitcast(FP8X4),
-                    rhs_scale=x_plane[:, j0:j1],
+                    rhs=x_codes[:, c0 : c0 + width].bitcast(FP8X4),
+                    rhs_scale=x_plane[:, c0 : c0 + width],
                     start=True,
                     stop=True,
                 )
-                nc.scalar.copy(a_sb[t][:, j0:j1], acc[:])
-        for t in range(PACK):
+                c0 = c0 + width
+            nc.scalar.copy(a_sb[t][:, j0:j1], acc[:])
+
+        first = [keep.tile([P, 2, O], F32, name=f"first{u}") for u in range(2)]
+        second = [keep.tile([P, 2, O], F32, name=f"second{u}") for u in range(2)]
+        for t, (j0, j1) in pieces:
             u, v = divmod(t, 2)
-            for j0, j1 in spans[t]:
-                nc.vector.tensor_copy(boards[t][:].indirect(board_list[:, j0 // 16 : j1 // 16]), a_sb[t][:, j0:j1])
-            nc.scalar.activation(
-                out=first[u][:, v, :], in_=boards[t][:].indirect(first_list[:]), func=COPY, scale=sa_sb[:, t : t + 1]
-            )
-            nc.scalar.activation(
-                out=second[u][:, v, :], in_=boards[t][:].indirect(second_list[:]), func=COPY, scale=sb_sb[:, t : t + 1]
-            )
+            nc.vector.tensor_copy(boards[t][:].indirect(board_list[:, j0 // 16 : j1 // 16]), a_sb[t][:, j0:j1])
+            if j1 == J:
+                nc.scalar.activation(
+                    out=first[u][:, v, :],
+                    in_=boards[t][:].indirect(first_list[:]),
+                    func=COPY,
+                    scale=sa_sb[:, t : t + 1],
+                )
+                nc.scalar.activation(
+                    out=second[u][:, v, :],
+                    in_=boards[t][:].indirect(second_list[:]),
+                    func=COPY,
+                    scale=sb_sb[:, t : t + 1],
+                )
 
         hid = keep.tile([P, O * PACK], BF16, name="hid", tag=f"a_sb{PACK - 1}", align_bytes=64)
 
@@ -172,12 +183,13 @@ def tile_picked_tokens_codes_one_boardpair_one_plain_kernel(
                 out=h_codes[:, o0:o1].bitcast(FP8X4), scales=h_plane[:, o0:o1], in_=hid[:, o0 * PACK : o1 * PACK]
             )
 
-        out_rows = out.rearrange("(b p) o -> p b o", p=P)
+        y_sb = [keep.tile([P, O], F32, name=f"y_sb{b}") for b in range(N // P)]
+        copies = [nc.scalar.copy, nc.vector.tensor_copy]
         for h, (o0, o1) in enumerate(halves):
-            y = psum.tile([P, N // P, o1 - o0], F32, name=f"y{h}")
             for b in range(N // P):
+                y = psum.tile([P, o1 - o0], F32, name=f"y{h}_{b}", tag=f"bank{2 * h + b}")
                 nc.tensor.matmul_mx(
-                    out=y[:, b, :],
+                    out=y[:],
                     lhsT=wb_codes[:, b * P : (b + 1) * P].bitcast(FP8X4),
                     lhsT_scale=wb_plane[:, b * P : (b + 1) * P],
                     rhs=h_codes[:, o0:o1].bitcast(FP8X4),
@@ -185,10 +197,6 @@ def tile_picked_tokens_codes_one_boardpair_one_plain_kernel(
                     start=True,
                     stop=True,
                 )
-            y_sb = keep.tile([P, N // P, o1 - o0], F32, name=f"y_sb{h}")
-            if h == 0:
-                nc.scalar.copy(y_sb[:], y[:])
-                nc.scalar.dma_start(out_rows[:, :, o0:o1], y_sb[:])
-            else:
-                nc.vector.tensor_copy(y_sb[:], y[:])
-                nc.sync.dma_start(out_rows[:, :, o0:o1], y_sb[:])
+                copies[b](y_sb[b][:, o0:o1], y[:])
+        nc.scalar.dma_start(out[0:P, :], y_sb[0][:])
+        nc.sync.dma_start(out[P : 2 * P, :], y_sb[1][:])

@@ -38,7 +38,7 @@ def tile_picked_tokens_codes_one_boardpair_one_plain_kernel(
         sa_sb = keep.tile([P, PACK], F32, name="sa_sb")
         sb_sb = keep.tile([P, PACK], F32, name="sb_sb")
         tables = [keep.tile([P, F], F32, name=f"table{t}") for t in range(PACK)]
-        xt_word_table = keep.tile([P, T], I32, name="xt_word_table")
+        xt_word_table = keep.tile([P, T], I32, name="xt_word_table", tag="xt_words", align_bytes=64)
         xt_scale_table = keep.tile([P, T], U8, name="xt_scale_table")
         wb_codes = keep.tile([P, N], I32, name="wb_codes", align_bytes=64)
         wb_plane = keep.tile([P, N], U8, name="wb_plane", align_bytes=64)
@@ -47,7 +47,7 @@ def tile_picked_tokens_codes_one_boardpair_one_plain_kernel(
         nc.gpsimd.memset(xt_scale_table[:].bitcast(I32), 0)
         nc.gpsimd.memset(wb_plane[:].bitcast(I32), 0)
         for t in range(PACK):
-            nc.vector.memset(boards[t][:], 0.0)
+            nc.gpsimd.memset(boards[t][:], 0.0)
 
         ua_rows = ua.rearrange("(p t) f -> p t f", t=PACK)
         xt_scale_rows = xt_scales[0].bitcast(I32)
@@ -80,7 +80,7 @@ def tile_picked_tokens_codes_one_boardpair_one_plain_kernel(
         wc = [keep.tile([P, 2, R], BF16, name=f"wc{e}") for e in range(2)]
         grouped = [keep.tile([P, 2 * P * PACK], BF16, name=f"grouped{u}", align_bytes=64) for u in range(2)]
         w_codes = [keep.tile([P, 2 * P], U32, name=f"w_codes{u}", align_bytes=64) for u in range(2)]
-        w_plane = [keep.tile([P, 2 * P], U8, name=f"w_plane{u}", align_bytes=64) for u in range(2)]
+        w_plane = [keep.tile([P, 2 * P], U8, name="w_plane0", align_bytes=64)]
 
         def gather_w(j):
             nc.scalar.activation(
@@ -121,16 +121,20 @@ def tile_picked_tokens_codes_one_boardpair_one_plain_kernel(
             nc.vector.tensor_copy(
                 x_codes[:, j0:j1], xt_word_table[:].bitcast(U32).indirect(token_list[:, j0 // 16 : j1 // 16])
             )
-        quantize_w(2, 4)
 
-        pieces = [(0, head), (1, head), (0, rest), (1, rest), (2, whole), (3, whole)]
+        w_plane.append(keep.tile([P, 2 * P], U8, name="w_plane1", tag="xt_words", align_bytes=64))
+        quantize_w(2, 4)
         widths = {head: [128], rest: [128, 256], whole: [512]}
-        a_sb = [keep.tile([P, J], F32, name=f"a_sb{t}", tag=f"a_sb{t}", align_bytes=64) for t in range(PACK)]
-        for bank, (t, (j0, j1)) in enumerate(pieces):
+        banks = {(0, head): 0, (1, head): 1, (0, rest): 2, (1, rest): 3, (2, whole): 4, (3, whole): 5}
+        first = [keep.tile([P, 2, O], F32, name=f"first{u}") for u in range(2)]
+        second = [keep.tile([P, 2, O], F32, name=f"second{u}") for u in range(2)]
+
+        def product(t, span):
             u, v = divmod(t, 2)
-            acc = psum.tile([P, j1 - j0], F32, name=f"acc{bank}", tag=f"bank{bank}")
+            j0, j1 = span
+            acc = psum.tile([P, j1 - j0], F32, name=f"acc{t}_{j0}", tag=f"bank{banks[(t, span)]}")
             c0 = j0
-            for width in widths[(j0, j1)]:
+            for width in widths[span]:
                 nc.tensor.matmul_mx(
                     out=acc[:, c0 - j0 : c0 - j0 + width],
                     lhsT=w_codes[u][:, v * P : (v + 1) * P].bitcast(FP8X4),
@@ -141,28 +145,35 @@ def tile_picked_tokens_codes_one_boardpair_one_plain_kernel(
                     stop=True,
                 )
                 c0 = c0 + width
-            nc.scalar.copy(a_sb[t][:, j0:j1], acc[:])
+            a_sb = keep.tile([P, j1 - j0], F32, name=f"a_sb{t}_{j0}", tag=f"a_sb{t}_{j0}", align_bytes=64)
+            nc.scalar.copy(a_sb[:], acc[:])
+            return a_sb
 
-        first = [keep.tile([P, 2, O], F32, name=f"first{u}") for u in range(2)]
-        second = [keep.tile([P, 2, O], F32, name=f"second{u}") for u in range(2)]
-        for t, (j0, j1) in pieces:
+        def scatter(t, span, a_sb):
+            nc.vector.tensor_copy(boards[t][:].indirect(board_list[:, span[0] // 16 : span[1] // 16]), a_sb[:])
+
+        def look_up(t):
             u, v = divmod(t, 2)
-            nc.vector.tensor_copy(boards[t][:].indirect(board_list[:, j0 // 16 : j1 // 16]), a_sb[t][:, j0:j1])
-            if j1 == J:
-                nc.scalar.activation(
-                    out=first[u][:, v, :],
-                    in_=boards[t][:].indirect(first_list[:]),
-                    func=COPY,
-                    scale=sa_sb[:, t : t + 1],
-                )
-                nc.scalar.activation(
-                    out=second[u][:, v, :],
-                    in_=boards[t][:].indirect(second_list[:]),
-                    func=COPY,
-                    scale=sb_sb[:, t : t + 1],
-                )
+            nc.scalar.activation(
+                out=first[u][:, v, :], in_=boards[t][:].indirect(first_list[:]), func=COPY, scale=sa_sb[:, t : t + 1]
+            )
+            nc.scalar.activation(
+                out=second[u][:, v, :], in_=boards[t][:].indirect(second_list[:]), func=COPY, scale=sb_sb[:, t : t + 1]
+            )
 
-        hid = keep.tile([P, O * PACK], BF16, name="hid", tag=f"a_sb{PACK - 1}", align_bytes=64)
+        heads = [product(t, head) for t in range(2)]
+        rests = [product(t, rest) for t in range(2)]
+        for t in range(2):
+            scatter(t, head, heads[t])
+        wholes = [product(t, whole) for t in range(2, PACK)]
+        for t in range(2):
+            scatter(t, rest, rests[t])
+            look_up(t)
+        for t in range(2, PACK):
+            scatter(t, whole, wholes[t - 2])
+            look_up(t)
+
+        hid = keep.tile([P, O * PACK], BF16, name="hid", tag=f"a_sb{PACK - 1}_0", align_bytes=64)
 
         def larger(u, o0, o1):
             nc.vector.tensor_tensor(
@@ -198,5 +209,5 @@ def tile_picked_tokens_codes_one_boardpair_one_plain_kernel(
                     stop=True,
                 )
                 copies[b](y_sb[b][:, o0:o1], y[:])
-        nc.scalar.dma_start(out[0:P, :], y_sb[0][:])
-        nc.sync.dma_start(out[P : 2 * P, :], y_sb[1][:])
+                queue = nc.scalar if (h, b) == (1, 0) else nc.sync
+                queue.dma_start(out[b * P : (b + 1) * P, o0:o1], y_sb[b][:, o0:o1])

from contextlib import ExitStack

import concourse.mybir as mybir

K, J, R, T, F, O, C, N = 512, 512, 512, 2048, 2048, 256, 1024, 256
FLOPS = 2 * K * R * J + 2 * R * N * O

F32 = mybir.dt.float32
BF16 = mybir.dt.bfloat16
I32 = mybir.dt.int32
U32 = mybir.dt.uint32
U16 = mybir.dt.uint16
U8 = mybir.dt.uint8
FP8X4 = mybir.dt.float8_e4m3fn_x4
COPY = mybir.ActivationFunctionType.Copy
MAX = mybir.AluOpType.max

P = 128
PACK = 4
HEAD = 128


def tile_picked_tokens_codes_one_boardpair_one_plain_kernel(
    tc, xt_words, xt_scales, ua, ha, sa, sb, wb_words, wb_scales, offs, offs2, offs3, offs4, offs5, out
):
    nc = tc.nc
    with ExitStack() as ctx:
        keep = ctx.enter_context(tc.tile_pool(name="keep", bufs=1))
        psum = ctx.enter_context(tc.psum_pool(name="psum", bufs=1))

        token_list = keep.tile([P, J // 16], U16, name="token_list")
        code_list = keep.tile([P, R // 16], U16, name="code_list")
        board_list = keep.tile([P, J // 16], U16, name="board_list")
        first_list = keep.tile([P, O // 16], U16, name="first_list")
        second_list = keep.tile([P, O // 16], U16, name="second_list")

        ha_sb = keep.tile([P, PACK], F32, name="ha_sb")
        sa_sb = keep.tile([P, PACK], F32, name="sa_sb")
        sb_sb = keep.tile([P, PACK], F32, name="sb_sb")
        tables = [keep.tile([P, F], F32, name=f"table{t}") for t in range(PACK)]
        xt_word_table = keep.tile([P, T], I32, name="xt_word_table", tag="xt_words", align_bytes=64)
        xt_scale_table = keep.tile([P, T], U8, name="xt_scale_table")
        wb_codes = keep.tile([P, N], I32, name="wb_codes", align_bytes=64)
        wb_plane = keep.tile([P, N], U8, name="wb_plane", align_bytes=64)
        boards = [keep.tile([P, C], F32, name=f"board{t}") for t in range(PACK)]

        nc.gpsimd.memset(xt_scale_table[:].bitcast(I32), 0)
        nc.gpsimd.memset(wb_plane[:].bitcast(I32), 0)
        for t in range(PACK):
            nc.gpsimd.memset(boards[t][:], 0.0)

        ua_rows = ua.rearrange("(p t) f -> p t f", t=PACK)
        xt_scale_rows = xt_scales[0].bitcast(I32)
        wb_scale_rows = wb_scales[0].bitcast(I32)

        nc.sync.dma_start(tables[0][:], ua_rows[:, 0, :])
        nc.sync.dma_start(code_list[:], offs2)
        nc.scalar.dma_start(ha_sb[:], ha.rearrange("(p t) one -> p (t one)", t=PACK))
        nc.sync.dma_start(token_list[:], offs)
        nc.sync.dma_start(xt_scale_table[0:P:8, :].bitcast(I32), xt_scale_rows)
        for t in range(1, PACK):
            nc.sync.dma_start(tables[t][:], ua_rows[:, t, :])
        nc.sync.dma_start(xt_word_table[:], xt_words[0].rearrange("p c t -> p (c t)").bitcast(I32))
        nc.sync.dma_start(board_list[:], offs3)
        nc.sync.dma_start(first_list[:], offs4)
        nc.sync.dma_start(second_list[:], offs5)
        nc.sync.dma_start(sa_sb[:], sa.rearrange("(p t) one -> p (t one)", t=PACK))
        nc.sync.dma_start(sb_sb[:], sb.rearrange("(p t) one -> p (t one)", t=PACK))
        nc.sync.dma_start(wb_codes[:], wb_words[0].rearrange("p n t -> p (n t)").bitcast(I32))
        for i in range(4):
            nc.sync.dma_start(wb_plane[i:P:32, :].bitcast(I32), wb_scale_rows[i:16:4, :])

        x_scales = keep.tile([P, J], U8, name="x_scales")
        nc.vector.tensor_copy(x_scales[:], xt_scale_table[:].indirect(token_list[:]))
        x_plane = keep.tile([P, J], U8, name="x_plane", align_bytes=64)
        nc.vector.tensor_copy(x_plane[:], x_scales[:])
        for i in range(1, 4):
            nc.gpsimd.dma_start(x_plane[i:P:32, :].bitcast(I32), x_scales[8 * i : P : 32, :].bitcast(I32))

        wc = [keep.tile([P, 2, R], BF16, name=f"wc{e}") for e in range(2)]
        grouped = [keep.tile([P, 2 * P * PACK], BF16, name=f"grouped{u}", align_bytes=64) for u in range(2)]
        w_codes = [keep.tile([P, 2 * P], U32, name=f"w_codes{u}", align_bytes=64) for u in range(2)]
        w_plane = [keep.tile([P, 2 * P], U8, name="w_plane0", align_bytes=64)]

        def gather_w(j):
            nc.scalar.activation(
                out=wc[j // 2][:, j % 2, :],
                in_=tables[j][:].indirect(code_list[:]),
                func=COPY,
                scale=ha_sb[:, j : j + 1],
            )

        def weave(copy, e, t0, t1):
            u, v = divmod(t0, 2)
            words = grouped[u][:, v * P * PACK : (v + t1 - t0) * P * PACK].rearrange("p (t m j) -> p t m j", m=P, j=PACK)
            copy(words[:, :, :, 2 * e : 2 * e + 2], wc[e][:].rearrange("p j (m t) -> p t m j", t=PACK)[:, t0:t1])

        def quantize_w(t0, t1):
            u, v = divmod(t0, 2)
            nc.vector.quantize_mx(
                out=w_codes[u][:, v * P : (v + t1 - t0) * P].bitcast(FP8X4),
                scales=w_plane[u][:, v * P : (v + t1 - t0) * P],
                in_=grouped[u][:, v * P * PACK : (v + t1 - t0) * P * PACK],
            )

        gather_w(0)
        gather_w(1)
        weave(nc.vector.tensor_copy, 0, 0, 2)
        weave(nc.vector.tensor_copy, 0, 2, 4)
        gather_w(2)
        gather_w(3)
        weave(nc.vector.tensor_copy, 1, 0, 1)
        weave(nc.vector.tensor_copy, 1, 1, 2)
        weave(nc.scalar.copy, 1, 2, 4)
        quantize_w(0, 1)
        quantize_w(1, 2)

        head, rest, whole = (0, HEAD), (HEAD, J), (0, J)
        x_codes = keep.tile([P, J], U32, name="x_codes", align_bytes=64)
        for j0, j1 in (head, rest):
            nc.vector.tensor_copy(
                x_codes[:, j0:j1], xt_word_table[:].bitcast(U32).indirect(token_list[:, j0 // 16 : j1 // 16])
            )

        w_plane.append(keep.tile([P, 2 * P], U8, name="w_plane1", tag="xt_words", align_bytes=64))
        quantize_w(2, 4)
        widths = {head: [128], rest: [128, 256], whole: [512]}
        banks = {(0, head): 0, (1, head): 1, (0, rest): 2, (1, rest): 3, (2, whole): 4, (3, whole): 5}
        first = [keep.tile([P, 2, O], F32, name=f"first{u}") for u in range(2)]
        second = [keep.tile([P, 2, O], F32, name=f"second{u}") for u in range(2)]

        def product(t, span):
            u, v = divmod(t, 2)
            j0, j1 = span
            acc = psum.tile([P, j1 - j0], F32, name=f"acc{t}_{j0}", tag=f"bank{banks[(t, span)]}")
            c0 = j0
            for width in widths[span]:
                nc.tensor.matmul_mx(
                    out=acc[:, c0 - j0 : c0 - j0 + width],
                    lhsT=w_codes[u][:, v * P : (v + 1) * P].bitcast(FP8X4),
                    lhsT_scale=w_plane[u][:, v * P : (v + 1) * P],
                    rhs=x_codes[:, c0 : c0 + width].bitcast(FP8X4),
                    rhs_scale=x_plane[:, c0 : c0 + width],
                    start=True,
                    stop=True,
                )
                c0 = c0 + width
            a_sb = keep.tile([P, j1 - j0], F32, name=f"a_sb{t}_{j0}", tag=f"a_sb{t}_{j0}", align_bytes=64)
            nc.scalar.copy(a_sb[:], acc[:])
            return a_sb

        def scatter(t, span, a_sb):
            nc.vector.tensor_copy(boards[t][:].indirect(board_list[:, span[0] // 16 : span[1] // 16]), a_sb[:])

        def look_up(t):
            u, v = divmod(t, 2)
            nc.scalar.activation(
                out=first[u][:, v, :], in_=boards[t][:].indirect(first_list[:]), func=COPY, scale=sa_sb[:, t : t + 1]
            )
            nc.scalar.activation(
                out=second[u][:, v, :], in_=boards[t][:].indirect(second_list[:]), func=COPY, scale=sb_sb[:, t : t + 1]
            )

        heads = [product(t, head) for t in range(2)]
        rests = [product(t, rest) for t in range(2)]
        for t in range(2):
            scatter(t, head, heads[t])
        wholes = [product(t, whole) for t in range(2, PACK)]
        for t in range(2):
            scatter(t, rest, rests[t])
            look_up(t)
        for t in range(2, PACK):
            scatter(t, whole, wholes[t - 2])
            look_up(t)

        hid = keep.tile([P, O * PACK], BF16, name="hid", tag=f"a_sb{PACK - 1}_0", align_bytes=64)

        def larger(u, o0, o1):
            nc.vector.tensor_tensor(
                hid[:, o0 * PACK : o1 * PACK].rearrange("p (o t) -> p o t", t=PACK)[:, :, 2 * u : 2 * u + 2],
                first[u][:, :, o0:o1].rearrange("p v o -> p o v"),
                second[u][:, :, o0:o1].rearrange("p v o -> p o v"),
                MAX,
            )

        halves = [(0, O // 2), (O // 2, O)]
        larger(0, 0, O)
        for o0, o1 in halves:
            larger(1, o0, o1)
        h_codes = keep.tile([P, O], U32, name="h_codes", align_bytes=64)
        h_plane = keep.tile([P, O], U8, name="h_plane", align_bytes=64)
        for o0, o1 in halves:
            nc.vector.quantize_mx(
                out=h_codes[:, o0:o1].bitcast(FP8X4), scales=h_plane[:, o0:o1], in_=hid[:, o0 * PACK : o1 * PACK]
            )

        y_sb = [keep.tile([P, O], F32, name=f"y_sb{b}") for b in range(N // P)]
        copies = [nc.scalar.copy, nc.vector.tensor_copy]
        for h, (o0, o1) in enumerate(halves):
            for b in range(N // P):
                y = psum.tile([P, o1 - o0], F32, name=f"y{h}_{b}", tag=f"bank{2 * h + b}")
                nc.tensor.matmul_mx(
                    out=y[:],
                    lhsT=wb_codes[:, b * P : (b + 1) * P].bitcast(FP8X4),
                    lhsT_scale=wb_plane[:, b * P : (b + 1) * P],
                    rhs=h_codes[:, o0:o1].bitcast(FP8X4),
                    rhs_scale=h_plane[:, o0:o1],
                    start=True,
                    stop=True,
                )
                copies[b](y_sb[b][:, o0:o1], y[:])
                queue = nc.scalar if (h, b) == (1, 0) else nc.sync
                queue.dma_start(out[b * P : (b + 1) * P, o0:o1], y_sb[b][:, o0:o1])
